import numpy as np
import ml_dtypes


def mxq(x, axis, fmt="e4m3"):
    dtype, down = {"e4m3": (ml_dtypes.float8_e4m3fn, 7), "e5m2": (ml_dtypes.float8_e5m2, 14)}[fmt]
    v = np.moveaxis(np.asarray(x, np.float32).astype(ml_dtypes.bfloat16).astype(np.float64), axis, -1)
    blocks = v.reshape(v.shape[:-1] + (-1, 32))
    amax = np.abs(blocks).max(-1, keepdims=True)
    byte = np.maximum(np.where(amax > 0, np.frexp(amax)[1] - 1 + 127, 0) - down, 1)
    scale = np.exp2(byte - 127.0)
    codes = (blocks / scale).astype(np.float32).astype(dtype).astype(np.float64)
    return np.moveaxis((codes * scale).reshape(v.shape), -1, axis)


WIDE = False


def mx_kscale(k):
    if not WIDE:
        return np.ones(k)
    levels = np.array([10, -10, 5, -5, 0])
    if k % 512:
        return np.exp2(np.random.permutation(np.resize(levels, k // 32))).repeat(32)
    a = np.empty((k // 512, 16))
    for p in range(k // 512):
        a[p, :8] = np.random.permutation(np.resize(levels, 8))
        for g in range(8):
            far = levels[np.abs(levels - a[p, g]) >= 10]
            a[p, g + 8] = far[np.random.randint(len(far))]
    return np.exp2(a.ravel()).repeat(32)


def f64(x):
    return np.asarray(x).astype(np.float64)


def striped(idx):
    return np.tile(idx.reshape(-1, 16).T, (8, 1)).astype(np.uint16)


def unstriped(offs):
    return offs[:16].T.reshape(-1).astype(np.int64)


def striped8(idx):
    return np.concatenate([x.reshape(-1, 16).T for x in idx]).astype(np.uint16)


def runs(offs, k):
    lists = np.stack([offs[16 * r : 16 * r + 16].T.reshape(-1) for r in range(8)]).astype(np.int64)
    return lists[np.arange(k) % 512 // 64]


def pack_weight(w):
    k, n = w.shape
    w = f64(np.asarray(w, np.float32).astype(ml_dtypes.bfloat16)).reshape(k // 32, 32, n)
    amax = np.abs(w).max(1)
    byte = np.clip(np.where(amax > 0, np.frexp(amax)[1] - 1 + 127 - 7, 1), 1, 254)
    scaled = (w * np.exp2(127.0 - byte)[:, None, :]).reshape(k, n).astype(np.float32)
    words = np.ascontiguousarray(scaled.reshape(k // 512, 128, 4, n).transpose(0, 1, 3, 2)).astype(ml_dtypes.float8_e4m3fn).view(np.uint8)
    return words, np.ascontiguousarray(byte.astype(np.uint8).reshape(k // 512, 16, n))


def unpack_weight(words, scales):
    g, p, n, _ = words.shape
    vals = np.ascontiguousarray(words).view(ml_dtypes.float8_e4m3fn).astype(np.float64) * np.repeat(np.exp2(scales.astype(np.float64) - 127.0), 8, axis=1)[..., None]
    return vals.transpose(0, 1, 3, 2).reshape(g * 512, n)

def planes(y):
    n, m = y.shape
    v = y.astype(np.float32).astype(ml_dtypes.bfloat16).astype(np.float64).reshape(n // 32, 32, m)
    top = np.abs(v).max(1)
    byte = np.clip(np.where(top > 0, np.frexp(top)[1] - 1 + 127 - 7, 1), 1, 254)
    codes = (v * np.exp2(127.0 - byte)[:, None, :]).reshape(n, m).astype(np.float32).astype(ml_dtypes.float8_e4m3fn).view(np.uint8)
    words = codes.reshape(n // 512, 128, 4, m).transpose(0, 1, 3, 2)
    return np.ascontiguousarray(words), np.ascontiguousarray(byte.astype(np.uint8).reshape(n // 512, 16, m))


K, T, S, V, H, J, W = 512, 2048, 512, 512, 512, 512, 256


def setup_inputs():
    n = np.random.standard_normal
    s = mx_kscale(K)[:, None]
    u = mx_kscale(S)
    packed_xT = pack_weight(n((K, T)) * s)
    packed_w1 = pack_weight(n((K, H)) / np.sqrt(K) / s)
    packed_w2 = pack_weight(n((K, H)) / np.sqrt(K) / s)
    perm = np.random.permutation(V)
    return {
        "x_words": packed_xT[0],
        "x_scales": packed_xT[1],
        "w1_words": packed_w1[0],
        "w1_scales": packed_w1[1],
        "w2_words": packed_w2[0],
        "w2_scales": packed_w2[1],
        "tab": n((H, J)).astype(np.float32),
        "ga": (np.random.uniform(0.5, 1.5, (H, 1)) * u[:, None]).astype(np.float32),
        "gb": (np.random.uniform(0.5, 1.5, (H, 1)) / u[:, None]).astype(np.float32),
        "offs": striped8(np.random.randint(0, T, (8, S))),
        "two": striped(np.random.permutation(T)[:V]),
        "n1": striped(np.random.randint(0, J, S)),
        "n2": striped(np.random.randint(0, J, S)),
        "n3": striped(np.random.permutation(S)),
        "n4": striped(np.random.permutation(V)),
        "n5": striped(np.random.permutation(V)),
        "n6": striped(perm[:W]),
        "n7": striped(perm[W:]),
        "n8": striped(np.random.permutation(V)),
    }


def reference(x_words, x_scales, w1_words, w1_scales, w2_words, w2_scales, tab, ga, gb, offs, two, n1, n2, n3, n4, n5, n6, n7, n8):
    xq = unpack_weight(x_words, x_scales)[np.arange(K)[:, None], runs(offs, K)]
    a = unpack_weight(w1_words, w1_scales).T @ xq
    z = f64(ga) * (a[:, unstriped(n3)] * f64(tab)[:, unstriped(n1)] + f64(tab)[:, unstriped(n2)])
    x_two = unpack_weight(x_words, x_scales)[:, unstriped(two)]
    b = unpack_weight(w2_words, w2_scales).T @ x_two
    z2 = f64(gb) * (b * (b[:, unstriped(n4)] - b[:, unstriped(n5)]))
    s = 0.0625 * ((mxq(z, 0, "e4m3").T @ mxq(z2, 0, "e4m3")))
    pa = s[:, unstriped(n6)]
    pb = s[:, unstriped(n7)]
    ra = pa - (0.5 * pb)
    ds = s.copy()
    ds[:, unstriped(n7)] = ra
    out_0 = ds - (0.5 * ds[:, unstriped(n8)])
    return (out_0,) + planes(out_0)

@@ -1,0 +1,241 @@
+from contextlib import ExitStack
+
+import concourse.mybir as mybir
+
+K, T, S, V, H, J, W = 512, 2048, 512, 512, 512, 512, 256
+FLOPS = 2 * K * H * S + 2 * K * H * V + 2 * H * S * V
+
+F32 = mybir.dt.float32
+BF16 = mybir.dt.bfloat16
+I32 = mybir.dt.int32
+U32 = mybir.dt.uint32
+U16 = mybir.dt.uint16
+U8 = mybir.dt.uint8
+FP8X4 = mybir.dt.float8_e4m3fn_x4
+COPY = mybir.ActivationFunctionType.Copy
+MULT = mybir.AluOpType.mult
+ADD = mybir.AluOpType.add
+
+P = 128
+PACK = 4
+QUAD = 32
+SPARE = 8
+WIDE = 512 + SPARE
+
+
+def tile_picked_hkqkindawindfoldd_none_po_kernel(
+    tc, x_words, x_scales, w1_words, w1_scales, w2_words, w2_scales, tab, ga, gb,
+    offs, two, n1, n2, n3, n4, n5, n6, n7, n8, out_0, out_1, out_2,
+):
+    nc = tc.nc
+    with ExitStack() as ctx:
+        keep = ctx.enter_context(tc.tile_pool(name="keep", bufs=1))
+        psum = ctx.enter_context(tc.psum_pool(name="psum", bufs=1))
+
+        def load_list(src, name):
+            lst = keep.tile(list(src.shape), U16, name=name)
+            nc.sync.dma_start(lst[:], src)
+            return lst
+
+        def words_of(packed):
+            return packed[0].rearrange("p n t -> p (n t)").bitcast(I32)
+
+        def zeroed(width, name):
+            plane = keep.tile([P, width], U8, name=name, align_bytes=64)
+            nc.vector.memset(plane[:].bitcast(I32), 0)
+            return plane
+
+        def load_scales(plane, scales):
+            for q in range(4):
+                nc.gpsimd.dma_start(
+                    plane[QUAD * q : QUAD * q + 4, :].bitcast(I32), scales[0, 4 * q : 4 * q + 4, :].bitcast(I32)
+                )
+
+        def deal(raw, dtype, name):
+            dealt = keep.tile([P, H], dtype, name=name, align_bytes=64)
+            nc.vector.tensor_copy(
+                dealt[:].rearrange("p (t m) -> p m t", t=PACK), raw[:].rearrange("p (m t) -> p m t", t=PACK)
+            )
+            return dealt
+
+        xs = zeroed(T, "xs")
+        ws1_raw = zeroed(H, "ws1_raw")
+        ws2_raw = zeroed(H, "ws2_raw")
+        x_plane = zeroed(S + V, "x_plane")
+
+        tab_rows = tab.rearrange("(p t) c -> p t c", t=PACK)
+        tabs = [keep.tile([P, WIDE], F32, name=f"tab{t}") for t in range(PACK)]
+        w1_raw = keep.tile([P, H], U32, name="w1_raw")
+        w2_raw = keep.tile([P, H], U32, name="w2_raw")
+        xw = keep.tile([P, T], U32, name="xw", align_bytes=64)
+        ga_sb = keep.tile([P, PACK], F32, name="ga_sb")
+        gb_sb = keep.tile([P, PACK], F32, name="gb_sb")
+
+        l_offs = load_list(offs, "l_offs")
+        nc.sync.dma_start(xs[0:P:8, :].bitcast(I32), x_scales[0].bitcast(I32))
+        l_n1 = load_list(n1, "l_n1")
+        for t in range(PACK):
+            nc.scalar.dma_start(tabs[t][:, 0:J], tab_rows[:, t, :])
+        nc.sync.dma_start(xw[:].bitcast(I32), words_of(x_words))
+        l_two = load_list(two, "l_two")
+        nc.sync.dma_start(w1_raw[:].bitcast(I32), words_of(w1_words))
+        nc.gpsimd.dma_start(ga_sb[:], ga.rearrange("(p t) o -> p (t o)", t=PACK))
+        load_scales(ws1_raw, w1_scales)
+        load_scales(ws2_raw, w2_scales)
+
+        xs_got = keep.tile([P, S + V], U8, name="xs_got", align_bytes=64)
+        nc.vector.tensor_copy(xs_got[:, 0:S], xs[:].indirect(l_offs[:]))
+        nc.vector.tensor_copy(xs_got[:, S : S + V], xs[:].indirect(l_two[:]))
+        for q in range(4):
+            nc.sync.dma_start(
+                x_plane[QUAD * q : QUAD * q + 4, :].bitcast(I32),
+                xs_got[QUAD * q : QUAD * (q + 1) : 8, :].bitcast(I32),
+            )
+        nc.sync.dma_start(w2_raw[:].bitcast(I32), words_of(w2_words))
+        nc.sync.dma_start(gb_sb[:], gb.rearrange("(p t) o -> p (t o)", t=PACK))
+        l_n3 = load_list(n3, "l_n3")
+        l_n5 = load_list(n5, "l_n5")
+        l_n4 = load_list(n4, "l_n4")
+        l_n2 = load_list(n2, "l_n2")
+        l_n7 = load_list(n7, "l_n7")
+        l_n6 = load_list(n6, "l_n6")
+        l_n8 = load_list(n8, "l_n8")
+
+        ws1 = deal(ws1_raw, U8, "ws1")
+        xw_offs = keep.tile([P, S], U32, name="xw_offs", align_bytes=64)
+        nc.vector.tensor_copy(xw_offs[:], xw[:].indirect(l_offs[:]))
+        w1 = deal(w1_raw, U32, "w1")
+        xw_two = keep.tile([P, V], U32, name="xw_two", align_bytes=64)
+        nc.vector.tensor_copy(xw_two[:], xw[:].indirect(l_two[:]))
+        w2 = deal(w2_raw, U32, "w2")
+        ws2 = deal(ws2_raw, U8, "ws2")
+
+        gtabs = [keep.tile([P, WIDE], F32, name=f"gtab{t}") for t in range(PACK)]
+        kinds = keep.tile([P, PACK, S], F32, name="kinds")
+        by_n1 = [kinds[:, t, :] for t in range(PACK)]
+        for t in range(PACK):
+            nc.gpsimd.tensor_scalar(gtabs[t][:, 0:J], tabs[t][:, 0:J], ga_sb[:, t : t + 1], 0.0, MULT, ADD)
+        for t in range(PACK):
+            nc.scalar.activation(by_n1[t], tabs[t][:].indirect(l_n1[:]), COPY)
+
+        a_banks = [psum.tile([P, S], F32, name=f"a_bank{t}", tag=f"as{t}") for t in range(PACK)]
+        for t in range(PACK):
+            rows = slice(P * t, P * (t + 1))
+            nc.tensor.matmul_mx(
+                out=a_banks[t][:], lhsT=w1[:, rows].bitcast(FP8X4), lhsT_scale=ws1[:, rows],
+                rhs=xw_offs[:].bitcast(FP8X4), rhs_scale=x_plane[:, 0:S], start=True, stop=True,
+            )
+        b_banks = [psum.tile([P, V], F32, name=f"b_bank{t}") for t in range(PACK)]
+        for t in range(PACK):
+            rows = slice(P * t, P * (t + 1))
+            nc.tensor.matmul_mx(
+                out=b_banks[t][:], lhsT=w2[:, rows].bitcast(FP8X4), lhsT_scale=ws2[:, rows],
+                rhs=xw_two[:].bitcast(FP8X4), rhs_scale=x_plane[:, S : S + V], start=True, stop=True,
+            )
+
+        gbs = [keep.tile([P, WIDE], F32, name=f"gb_b{t}") for t in range(PACK)]
+        gas = [keep.tile([P, WIDE], F32, name=f"ga_a{t}") for t in range(PACK)]
+        neg5 = keep.tile([P, PACK, V], F32, name="neg5")
+        diff = keep.tile([P, PACK, V], F32, name="diff")
+        prod = keep.tile([P, PACK, S], F32, name="prod")
+        z2 = keep.tile([P, PACK, V], F32, name="z2")
+
+        def a_side(t):
+            nc.scalar.activation(gas[t][:, 0:S], a_banks[t][:], COPY, scale=ga_sb[:, t : t + 1])
+            nc.vector.tensor_tensor(prod[:, t, :], gas[t][:].indirect(l_n3[:]), by_n1[t], MULT)
+
+        def b_side(t):
+            nc.scalar.activation(gbs[t][:, 0:V], b_banks[t][:], COPY, scale=gb_sb[:, t : t + 1])
+            nc.scalar.activation(neg5[:, t, :], gbs[t][:].indirect(l_n5[:]), COPY, scale=-1.0)
+            nc.vector.tensor_tensor(diff[:, t, :], gbs[t][:].indirect(l_n4[:]), neg5[:, t, :], ADD)
+            nc.vector.tensor_tensor(z2[:, t, :], b_banks[t][:], diff[:, t, :], MULT)
+
+        a_side(0)
+        for t in range(PACK):
+            if t + 1 < PACK:
+                a_side(t + 1)
+            b_side(t)
+
+        z2_bf = keep.tile([P, V * PACK], BF16, name="z2_bf", align_bytes=64)
+        nc.vector.tensor_copy(
+            z2_bf[:].rearrange("p (c i t) -> p c t i", i=4, t=PACK), z2[:].rearrange("p t (c i) -> p c t i", i=4)
+        )
+        z2_codes = keep.tile([P, V], U32, name="z2_codes", align_bytes=64)
+        z2_plane = keep.tile([P, V], U8, name="z2_plane", align_bytes=64)
+        nc.vector.quantize_mx(z2_codes[:].bitcast(FP8X4), z2_plane[:], z2_bf[:])
+
+        z_bf = keep.tile([P, S * PACK], BF16, name="z_bf", align_bytes=64)
+        z_view = z_bf[:].rearrange("p (u m t) -> p m t u", u=PACK, t=PACK)
+        prod_view = prod[:].rearrange("p t (m u) -> p m t u", u=PACK)
+        kinds_view = kinds[:].rearrange("p t (m u) -> p m t u", u=PACK)
+        for h in range(2):
+            for t in range(PACK):
+                nc.scalar.activation(
+                    kinds[:, t, W * h : W * (h + 1)], gtabs[t][:].indirect(l_n2[:, 16 * h : 16 * (h + 1)]), COPY
+                )
+            part = slice(64 * h, 64 * (h + 1))
+            nc.vector.tensor_tensor(z_view[:, part], prod_view[:, part], kinds_view[:, part], ADD)
+        z_codes = keep.tile([P, S], U32, name="z_codes", align_bytes=64)
+        z_plane = keep.tile([P, S], U8, name="z_plane", align_bytes=64)
+
+        s_banks = []
+        for t in range(PACK):
+            rows = slice(P * t, P * (t + 1))
+            nc.vector.quantize_mx(z_codes[:, rows].bitcast(FP8X4), z_plane[:, rows], z_bf[:, S * t : S * (t + 1)])
+            s_bank = psum.tile([P, V], F32, name=f"s_bank{t}", tag=f"as{t}")
+            nc.tensor.matmul_mx(
+                out=s_bank[:], lhsT=z_codes[:, rows].bitcast(FP8X4), lhsT_scale=z_plane[:, rows],
+                rhs=z2_codes[:].bitcast(FP8X4), rhs_scale=z2_plane[:], start=True, stop=True,
+            )
+            s_banks.append(s_bank)
+
+        res = keep.tile([P, PACK, V], F32, name="res")
+        out_rows = out_0.rearrange("(p t) v -> p t v", t=PACK)
+        dss = [keep.tile([P, V], F32, name=f"ds{t}") for t in range(PACK)]
+        pbs = [keep.tile([P, W], F32, name=f"pb{t}") for t in range(PACK)]
+        ras = [keep.tile([P, W], F32, name=f"ra{t}") for t in range(PACK)]
+        halves = [keep.tile([P, WIDE], F32, name=f"half{t}") for t in range(PACK)]
+
+        def pair_up(t):
+            if t == 0:
+                nc.scalar.activation(dss[t][:], s_banks[t][:], COPY, scale=0.0625)
+            else:
+                nc.vector.tensor_scalar(dss[t][:], s_banks[t][:], 0.0625, None, MULT)
+            nc.scalar.activation(pbs[t][:], dss[t][:].indirect(l_n7[:]), COPY, scale=-0.5)
+            nc.vector.tensor_tensor(ras[t][:], dss[t][:].indirect(l_n6[:]), pbs[t][:], ADD)
+
+        def finish(t, pieces):
+            nc.scalar.activation(dss[t][:].indirect(l_n7[:]), ras[t][:], COPY)
+            nc.vector.tensor_scalar(halves[t][:, 0:V], dss[t][:], -0.5, None, MULT)
+            width = V // pieces
+            for h in range(pieces):
+                cols = slice(width * h, width * (h + 1))
+                nc.vector.tensor_tensor(
+                    res[:, t, cols], halves[t][:].indirect(l_n8[:, width // 16 * h : width // 16 * (h + 1)]),
+                    dss[t][:, cols], ADD,
+                )
+            nc.sync.dma_start(out_rows[:, t, :], res[:, t, :])
+
+        pair_up(0)
+        for t in range(PACK):
+            if t + 1 < PACK:
+                pair_up(t + 1)
+            finish(t, 2 if t == PACK - 1 else 1)
+
+        o_bf = keep.tile([P, V * PACK], BF16, name="o_bf", align_bytes=64)
+        o_codes = keep.tile([P, V], U32, name="o_codes", align_bytes=64)
+        o_plane = keep.tile([P, V], U8, name="o_plane", align_bytes=64)
+        o_view = o_bf[:].rearrange("p (c i t) -> p c t i", i=4, t=PACK)
+        res_view = res[:].rearrange("p t (c i) -> p c t i", i=4)
+        out_words = out_1[0].rearrange("p n t -> p (n t)").bitcast(I32)
+        nc.scalar.copy(o_view[:, 0:64], res_view[:, 0:64])
+        nc.vector.tensor_copy(o_view[:, 64:128], res_view[:, 64:128])
+        for h in range(2):
+            cols = slice(W * h, W * (h + 1))
+            nc.vector.quantize_mx(
+                o_codes[:, cols].bitcast(FP8X4), o_plane[:, cols], o_bf[:, PACK * W * h : PACK * W * (h + 1)]
+            )
+            nc.sync.dma_start(out_words[:, cols], o_codes[:, cols].bitcast(I32))
+        for q in range(4):
+            eng = nc.scalar if q % 2 == 0 else nc.sync
+            eng.dma_start(out_2[0, 4 * q : 4 * q + 4, :].bitcast(I32), o_plane[QUAD * q : QUAD * q + 4, :].bitcast(I32))

@@ -40,32 +40,32 @@ def tile_picked_hkqkindawindfoldd_none_po_kernel(
         def words_of(packed):
             return packed[0].rearrange("p n t -> p (n t)").bitcast(I32)
 
-        def zeroed(width, name):
+        def zeroed(engine, width, name):
             plane = keep.tile([P, width], U8, name=name, align_bytes=64)
-            nc.vector.memset(plane[:].bitcast(I32), 0)
+            engine.memset(plane[:].bitcast(I32), 0)
             return plane
 
-        def load_scales(plane, scales):
+        def load_scales(queue, plane, scales):
             for q in range(4):
-                nc.gpsimd.dma_start(
+                queue.dma_start(
                     plane[QUAD * q : QUAD * q + 4, :].bitcast(I32), scales[0, 4 * q : 4 * q + 4, :].bitcast(I32)
                 )
 
-        def deal(raw, dtype, name):
-            dealt = keep.tile([P, H], dtype, name=name, align_bytes=64)
+        def deal(raw, dtype, name, tag):
+            dealt = keep.tile([P, H], dtype, name=name, tag=tag, align_bytes=64)
             nc.vector.tensor_copy(
                 dealt[:].rearrange("p (t m) -> p m t", t=PACK), raw[:].rearrange("p (m t) -> p m t", t=PACK)
             )
             return dealt
 
-        xs = zeroed(T, "xs")
-        ws1_raw = zeroed(H, "ws1_raw")
-        ws2_raw = zeroed(H, "ws2_raw")
-        x_plane = zeroed(S + V, "x_plane")
+        xs = zeroed(nc.gpsimd, T, "xs")
+        ws1_raw = zeroed(nc.vector, H, "ws1_raw")
+        ws2_raw = zeroed(nc.vector, H, "ws2_raw")
+        x_plane = zeroed(nc.vector, S + V, "x_plane")
 
         tab_rows = tab.rearrange("(p t) c -> p t c", t=PACK)
         tabs = [keep.tile([P, WIDE], F32, name=f"tab{t}") for t in range(PACK)]
-        w1_raw = keep.tile([P, H], U32, name="w1_raw")
+        w1_raw = keep.tile([P, H], U32, name="w1_raw", tag="w1_raw", align_bytes=64)
         w2_raw = keep.tile([P, H], U32, name="w2_raw")
         xw = keep.tile([P, T], U32, name="xw", align_bytes=64)
         ga_sb = keep.tile([P, PACK], F32, name="ga_sb")
@@ -74,16 +74,18 @@ def tile_picked_hkqkindawindfoldd_none_po_kernel(
         l_offs = load_list(offs, "l_offs")
         nc.sync.dma_start(xs[0:P:8, :].bitcast(I32), x_scales[0].bitcast(I32))
         l_n1 = load_list(n1, "l_n1")
-        for t in range(PACK):
-            nc.scalar.dma_start(tabs[t][:, 0:J], tab_rows[:, t, :])
-        nc.sync.dma_start(xw[:].bitcast(I32), words_of(x_words))
         l_two = load_list(two, "l_two")
-        nc.sync.dma_start(w1_raw[:].bitcast(I32), words_of(w1_words))
+        nc.scalar.dma_start(tabs[0][:, 0:J], tab_rows[:, 0, :])
+        nc.scalar.dma_start(xw[:].bitcast(I32), words_of(x_words))
+        for t in (1, 2):
+            nc.scalar.dma_start(tabs[t][:, 0:J], tab_rows[:, t, :])
         nc.gpsimd.dma_start(ga_sb[:], ga.rearrange("(p t) o -> p (t o)", t=PACK))
-        load_scales(ws1_raw, w1_scales)
-        load_scales(ws2_raw, w2_scales)
+        load_scales(nc.gpsimd, ws2_raw, w2_scales)
+        load_scales(nc.sync, ws1_raw, w1_scales)
+        nc.sync.dma_start(w1_raw[:].bitcast(I32), words_of(w1_words))
+        nc.sync.dma_start(tabs[3][:, 0:J], tab_rows[:, 3, :])
 
-        xs_got = keep.tile([P, S + V], U8, name="xs_got", align_bytes=64)
+        xs_got = keep.tile([P, S + V], U8, name="xs_got", tag="picked_bytes", align_bytes=64)
         nc.vector.tensor_copy(xs_got[:, 0:S], xs[:].indirect(l_offs[:]))
         nc.vector.tensor_copy(xs_got[:, S : S + V], xs[:].indirect(l_two[:]))
         for q in range(4):
@@ -92,8 +94,8 @@ def tile_picked_hkqkindawindfoldd_none_po_kernel(
                 xs_got[QUAD * q : QUAD * (q + 1) : 8, :].bitcast(I32),
             )
         nc.sync.dma_start(w2_raw[:].bitcast(I32), words_of(w2_words))
-        nc.sync.dma_start(gb_sb[:], gb.rearrange("(p t) o -> p (t o)", t=PACK))
         l_n3 = load_list(n3, "l_n3")
+        nc.sync.dma_start(gb_sb[:], gb.rearrange("(p t) o -> p (t o)", t=PACK))
         l_n5 = load_list(n5, "l_n5")
         l_n4 = load_list(n4, "l_n4")
         l_n2 = load_list(n2, "l_n2")
@@ -101,14 +103,14 @@ def tile_picked_hkqkindawindfoldd_none_po_kernel(
         l_n6 = load_list(n6, "l_n6")
         l_n8 = load_list(n8, "l_n8")
 
-        ws1 = deal(ws1_raw, U8, "ws1")
         xw_offs = keep.tile([P, S], U32, name="xw_offs", align_bytes=64)
         nc.vector.tensor_copy(xw_offs[:], xw[:].indirect(l_offs[:]))
-        w1 = deal(w1_raw, U32, "w1")
-        xw_two = keep.tile([P, V], U32, name="xw_two", align_bytes=64)
+        ws1 = deal(ws1_raw, U8, "ws1", "ws1")
+        w1 = deal(w1_raw, U32, "w1", "w1")
+        xw_two = keep.tile([P, V], U32, name="xw_two", tag="w1_raw", align_bytes=64)
         nc.vector.tensor_copy(xw_two[:], xw[:].indirect(l_two[:]))
-        w2 = deal(w2_raw, U32, "w2")
-        ws2 = deal(ws2_raw, U8, "ws2")
+        w2 = deal(w2_raw, U32, "w2", "w2")
+        ws2 = deal(ws2_raw, U8, "ws2", "picked_bytes")
 
         gtabs = [keep.tile([P, WIDE], F32, name=f"gtab{t}") for t in range(PACK)]
         kinds = keep.tile([P, PACK, S], F32, name="kinds")
@@ -141,7 +143,10 @@ def tile_picked_hkqkindawindfoldd_none_po_kernel(
         z2 = keep.tile([P, PACK, V], F32, name="z2")
 
         def a_side(t):
-            nc.scalar.activation(gas[t][:, 0:S], a_banks[t][:], COPY, scale=ga_sb[:, t : t + 1])
+            if t == 0:
+                nc.vector.tensor_scalar(gas[t][:, 0:S], a_banks[t][:], ga_sb[:, t : t + 1], None, MULT)
+            else:
+                nc.scalar.activation(gas[t][:, 0:S], a_banks[t][:], COPY, scale=ga_sb[:, t : t + 1])
             nc.vector.tensor_tensor(prod[:, t, :], gas[t][:].indirect(l_n3[:]), by_n1[t], MULT)
 
         def b_side(t):
@@ -168,52 +173,67 @@ def tile_picked_hkqkindawindfoldd_none_po_kernel(
         z_view = z_bf[:].rearrange("p (u m t) -> p m t u", u=PACK, t=PACK)
         prod_view = prod[:].rearrange("p t (m u) -> p m t u", u=PACK)
         kinds_view = kinds[:].rearrange("p t (m u) -> p m t u", u=PACK)
+        z_codes = keep.tile([P, S], U32, name="z_codes", align_bytes=64)
+        z_plane = keep.tile([P, S], U8, name="z_plane", align_bytes=64)
+        s_banks = []
         for h in range(2):
             for t in range(PACK):
                 nc.scalar.activation(
                     kinds[:, t, W * h : W * (h + 1)], gtabs[t][:].indirect(l_n2[:, 16 * h : 16 * (h + 1)]), COPY
                 )
             part = slice(64 * h, 64 * (h + 1))
-            nc.vector.tensor_tensor(z_view[:, part], prod_view[:, part], kinds_view[:, part], ADD)
-        z_codes = keep.tile([P, S], U32, name="z_codes", align_bytes=64)
-        z_plane = keep.tile([P, S], U8, name="z_plane", align_bytes=64)
-
-        s_banks = []
-        for t in range(PACK):
-            rows = slice(P * t, P * (t + 1))
-            nc.vector.quantize_mx(z_codes[:, rows].bitcast(FP8X4), z_plane[:, rows], z_bf[:, S * t : S * (t + 1)])
-            s_bank = psum.tile([P, V], F32, name=f"s_bank{t}", tag=f"as{t}")
-            nc.tensor.matmul_mx(
-                out=s_bank[:], lhsT=z_codes[:, rows].bitcast(FP8X4), lhsT_scale=z_plane[:, rows],
-                rhs=z2_codes[:].bitcast(FP8X4), rhs_scale=z2_plane[:], start=True, stop=True,
-            )
-            s_banks.append(s_bank)
+            for pair in range(2):
+                us = slice(2 * pair, 2 * pair + 2)
+                nc.vector.tensor_tensor(
+                    z_view[:, part, :, us], prod_view[:, part, :, us], kinds_view[:, part, :, us], ADD
+                )
+                for t in range(2 * pair, 2 * pair + 2) if h == 1 else ():
+                    rows = slice(P * t, P * (t + 1))
+                    nc.vector.quantize_mx(
+                        z_codes[:, rows].bitcast(FP8X4), z_plane[:, rows], z_bf[:, S * t : S * (t + 1)]
+                    )
+                    s_bank = psum.tile([P, V], F32, name=f"s_bank{t}", tag=f"as{t}")
+                    nc.tensor.matmul_mx(
+                        out=s_bank[:], lhsT=z_codes[:, rows].bitcast(FP8X4), lhsT_scale=z_plane[:, rows],
+                        rhs=z2_codes[:].bitcast(FP8X4), rhs_scale=z2_plane[:], start=True, stop=True,
+                    )
+                    s_banks.append(s_bank)
 
         res = keep.tile([P, PACK, V], F32, name="res")
         out_rows = out_0.rearrange("(p t) v -> p t v", t=PACK)
-        dss = [keep.tile([P, V], F32, name=f"ds{t}") for t in range(PACK)]
+        dss = [keep.tile([P, WIDE], F32, name=f"ds{t}") for t in range(PACK)]
         pbs = [keep.tile([P, W], F32, name=f"pb{t}") for t in range(PACK)]
-        ras = [keep.tile([P, W], F32, name=f"ra{t}") for t in range(PACK)]
+        pas = [keep.tile([P, W], F32, name=f"pa{t}") for t in range(PACK)]
         halves = [keep.tile([P, WIDE], F32, name=f"half{t}") for t in range(PACK)]
 
         def pair_up(t):
-            if t == 0:
-                nc.scalar.activation(dss[t][:], s_banks[t][:], COPY, scale=0.0625)
+            if t < 2:
+                nc.scalar.activation(dss[t][:, 0:V], s_banks[t][:], COPY, scale=0.0625)
             else:
-                nc.vector.tensor_scalar(dss[t][:], s_banks[t][:], 0.0625, None, MULT)
+                nc.vector.tensor_scalar(dss[t][:, 0:V], s_banks[t][:], 0.0625, None, MULT)
             nc.scalar.activation(pbs[t][:], dss[t][:].indirect(l_n7[:]), COPY, scale=-0.5)
-            nc.vector.tensor_tensor(ras[t][:], dss[t][:].indirect(l_n6[:]), pbs[t][:], ADD)
+            if t < 2:
+                nc.vector.tensor_tensor(pas[t][:], dss[t][:].indirect(l_n6[:]), pbs[t][:], ADD)
+            else:
+                nc.vector.tensor_copy(pas[t][:], dss[t][:].indirect(l_n6[:]))
 
         def finish(t, pieces):
-            nc.scalar.activation(dss[t][:].indirect(l_n7[:]), ras[t][:], COPY)
-            nc.vector.tensor_scalar(halves[t][:, 0:V], dss[t][:], -0.5, None, MULT)
-            width = V // pieces
-            for h in range(pieces):
-                cols = slice(width * h, width * (h + 1))
-                nc.vector.tensor_tensor(
-                    res[:, t, cols], halves[t][:].indirect(l_n8[:, width // 16 * h : width // 16 * (h + 1)]),
-                    dss[t][:, cols], ADD,
-                )
+            if t < 2:
+                nc.scalar.activation(dss[t][:].indirect(l_n7[:]), pas[t][:], COPY)
+            else:
+                nc.vector.tensor_tensor(dss[t][:].indirect(l_n7[:]), pas[t][:], pbs[t][:], ADD)
+            if t == 0:
+                nc.vector.tensor_scalar(halves[t][:, 0:V], dss[t][:, 0:V], -0.5, None, MULT)
+                nc.vector.tensor_tensor(res[:, t, :], halves[t][:].indirect(l_n8[:]), dss[t][:, 0:V], ADD)
+            else:
+                width = V // pieces
+                for h in range(pieces):
+                    cols = slice(width * h, width * (h + 1))
+                    nc.scalar.activation(
+                        halves[t][:, cols], dss[t][:].indirect(l_n8[:, width // 16 * h : width // 16 * (h + 1)]),
+                        COPY, scale=-0.5,
+                    )
+                    nc.vector.tensor_tensor(res[:, t, cols], dss[t][:, cols], halves[t][:, cols], ADD)
             nc.sync.dma_start(out_rows[:, t, :], res[:, t, :])
 
         pair_up(0)
@@ -237,5 +257,6 @@ def tile_picked_hkqkindawindfoldd_none_po_kernel(
             )
             nc.sync.dma_start(out_words[:, cols], o_codes[:, cols].bitcast(I32))
         for q in range(4):
-            eng = nc.scalar if q % 2 == 0 else nc.sync
-            eng.dma_start(out_2[0, 4 * q : 4 * q + 4, :].bitcast(I32), o_plane[QUAD * q : QUAD * q + 4, :].bitcast(I32))
+            nc.scalar.dma_start(
+                out_2[0, 4 * q : 4 * q + 4, :].bitcast(I32), o_plane[QUAD * q : QUAD * q + 4, :].bitcast(I32)
+            )

@@ -45,8 +45,8 @@ def tile_picked_hkqkindawindfoldd_none_po_kernel(
             engine.memset(plane[:].bitcast(I32), 0)
             return plane
 
-        def load_scales(queue, plane, scales):
-            for q in range(4):
+        def load_scales(queues, plane, scales):
+            for q, queue in enumerate(queues):
                 queue.dma_start(
                     plane[QUAD * q : QUAD * q + 4, :].bitcast(I32), scales[0, 4 * q : 4 * q + 4, :].bitcast(I32)
                 )
@@ -72,28 +72,30 @@ def tile_picked_hkqkindawindfoldd_none_po_kernel(
         gb_sb = keep.tile([P, PACK], F32, name="gb_sb")
 
         l_offs = load_list(offs, "l_offs")
+        l_two = load_list(two, "l_two")
         nc.sync.dma_start(xs[0:P:8, :].bitcast(I32), x_scales[0].bitcast(I32))
         l_n1 = load_list(n1, "l_n1")
-        l_two = load_list(two, "l_two")
+        nc.sync.dma_start(xw[:].bitcast(I32), words_of(x_words))
         nc.scalar.dma_start(tabs[0][:, 0:J], tab_rows[:, 0, :])
-        nc.scalar.dma_start(xw[:].bitcast(I32), words_of(x_words))
-        for t in (1, 2):
-            nc.scalar.dma_start(tabs[t][:, 0:J], tab_rows[:, t, :])
-        nc.gpsimd.dma_start(ga_sb[:], ga.rearrange("(p t) o -> p (t o)", t=PACK))
-        load_scales(nc.gpsimd, ws2_raw, w2_scales)
-        load_scales(nc.sync, ws1_raw, w1_scales)
+        nc.scalar.dma_start(ga_sb[:], ga.rearrange("(p t) o -> p (t o)", t=PACK))
+        load_scales([nc.scalar, nc.sync, nc.sync, nc.sync], ws1_raw, w1_scales)
+        load_scales([nc.gpsimd] * 4, ws2_raw, w2_scales)
         nc.sync.dma_start(w1_raw[:].bitcast(I32), words_of(w1_words))
-        nc.sync.dma_start(tabs[3][:, 0:J], tab_rows[:, 3, :])
+        for t in (1, 2):
+            nc.sync.dma_start(tabs[t][:, 0:J], tab_rows[:, t, :])
 
-        xs_got = keep.tile([P, S + V], U8, name="xs_got", tag="picked_bytes", align_bytes=64)
-        nc.vector.tensor_copy(xs_got[:, 0:S], xs[:].indirect(l_offs[:]))
-        nc.vector.tensor_copy(xs_got[:, S : S + V], xs[:].indirect(l_two[:]))
-        for q in range(4):
-            nc.sync.dma_start(
-                x_plane[QUAD * q : QUAD * q + 4, :].bitcast(I32),
-                xs_got[QUAD * q : QUAD * (q + 1) : 8, :].bitcast(I32),
-            )
+        def pick_scales(offsets, plane, name):
+            picked = keep.tile([P, S], U8, name=name, tag=name, align_bytes=64)
+            nc.vector.tensor_copy(picked[:], xs[:].indirect(offsets[:]))
+            for q in range(4):
+                nc.sync.dma_start(
+                    plane[QUAD * q : QUAD * q + 4, :].bitcast(I32), picked[QUAD * q : QUAD * (q + 1) : 8, :].bitcast(I32)
+                )
+
+        pick_scales(l_offs, x_plane[:, 0:S], "picked_bytes")
+        nc.sync.dma_start(tabs[3][:, 0:J], tab_rows[:, 3, :])
         nc.sync.dma_start(w2_raw[:].bitcast(I32), words_of(w2_words))
+        pick_scales(l_two, x_plane[:, S : S + V], "picked_by_two")
         l_n3 = load_list(n3, "l_n3")
         nc.sync.dma_start(gb_sb[:], gb.rearrange("(p t) o -> p (t o)", t=PACK))
         l_n5 = load_list(n5, "l_n5")
@@ -169,35 +171,35 @@ def tile_picked_hkqkindawindfoldd_none_po_kernel(
         z2_plane = keep.tile([P, V], U8, name="z2_plane", align_bytes=64)
         nc.vector.quantize_mx(z2_codes[:].bitcast(FP8X4), z2_plane[:], z2_bf[:])
 
-        z_bf = keep.tile([P, S * PACK], BF16, name="z_bf", align_bytes=64)
-        z_view = z_bf[:].rearrange("p (u m t) -> p m t u", u=PACK, t=PACK)
         prod_view = prod[:].rearrange("p t (m u) -> p m t u", u=PACK)
         kinds_view = kinds[:].rearrange("p t (m u) -> p m t u", u=PACK)
         z_codes = keep.tile([P, S], U32, name="z_codes", align_bytes=64)
         z_plane = keep.tile([P, S], U8, name="z_plane", align_bytes=64)
         s_banks = []
-        for h in range(2):
-            for t in range(PACK):
-                nc.scalar.activation(
-                    kinds[:, t, W * h : W * (h + 1)], gtabs[t][:].indirect(l_n2[:, 16 * h : 16 * (h + 1)]), COPY
+        for pair in range(2):
+            us = slice(2 * pair, 2 * pair + 2)
+            z_bf = keep.tile([P, 2 * S], BF16, name=f"z_bf{pair}", tag="z_bf", align_bytes=64)
+            z_view = z_bf[:].rearrange("p (u m t) -> p m t u", u=2, t=PACK)
+            if pair == 0:
+                for h in range(2):
+                    for t in range(PACK):
+                        nc.scalar.activation(
+                            kinds[:, t, W * h : W * (h + 1)], gtabs[t][:].indirect(l_n2[:, 16 * h : 16 * (h + 1)]), COPY
+                        )
+                    part = slice(64 * h, 64 * (h + 1))
+                    nc.vector.tensor_tensor(z_view[:, part], prod_view[:, part, :, us], kinds_view[:, part, :, us], ADD)
+            else:
+                nc.vector.tensor_tensor(z_view, prod_view[:, :, :, us], kinds_view[:, :, :, us], ADD)
+            for u in range(2):
+                t = 2 * pair + u
+                rows = slice(P * t, P * (t + 1))
+                nc.vector.quantize_mx(z_codes[:, rows].bitcast(FP8X4), z_plane[:, rows], z_bf[:, S * u : S * (u + 1)])
+                s_bank = psum.tile([P, V], F32, name=f"s_bank{t}", tag=f"as{t}")
+                nc.tensor.matmul_mx(
+                    out=s_bank[:], lhsT=z_codes[:, rows].bitcast(FP8X4), lhsT_scale=z_plane[:, rows],
+                    rhs=z2_codes[:].bitcast(FP8X4), rhs_scale=z2_plane[:], start=True, stop=True,
                 )
-            part = slice(64 * h, 64 * (h + 1))
-            for pair in range(2):
-                us = slice(2 * pair, 2 * pair + 2)
-                nc.vector.tensor_tensor(
-                    z_view[:, part, :, us], prod_view[:, part, :, us], kinds_view[:, part, :, us], ADD
-                )
-                for t in range(2 * pair, 2 * pair + 2) if h == 1 else ():
-                    rows = slice(P * t, P * (t + 1))
-                    nc.vector.quantize_mx(
-                        z_codes[:, rows].bitcast(FP8X4), z_plane[:, rows], z_bf[:, S * t : S * (t + 1)]
-                    )
-                    s_bank = psum.tile([P, V], F32, name=f"s_bank{t}", tag=f"as{t}")
-                    nc.tensor.matmul_mx(
-                        out=s_bank[:], lhsT=z_codes[:, rows].bitcast(FP8X4), lhsT_scale=z_plane[:, rows],
-                        rhs=z2_codes[:].bitcast(FP8X4), rhs_scale=z2_plane[:], start=True, stop=True,
-                    )
-                    s_banks.append(s_bank)
+                s_banks.append(s_bank)
 
         res = keep.tile([P, PACK, V], F32, name="res")
         out_rows = out_0.rearrange("(p t) v -> p t v", t=PACK)
@@ -207,22 +209,22 @@ def tile_picked_hkqkindawindfoldd_none_po_kernel(
         halves = [keep.tile([P, WIDE], F32, name=f"half{t}") for t in range(PACK)]
 
         def pair_up(t):
-            if t < 2:
+            if t < 3:
                 nc.scalar.activation(dss[t][:, 0:V], s_banks[t][:], COPY, scale=0.0625)
             else:
                 nc.vector.tensor_scalar(dss[t][:, 0:V], s_banks[t][:], 0.0625, None, MULT)
             nc.scalar.activation(pbs[t][:], dss[t][:].indirect(l_n7[:]), COPY, scale=-0.5)
-            if t < 2:
+            if t % 2 == 0:
                 nc.vector.tensor_tensor(pas[t][:], dss[t][:].indirect(l_n6[:]), pbs[t][:], ADD)
             else:
                 nc.vector.tensor_copy(pas[t][:], dss[t][:].indirect(l_n6[:]))
 
         def finish(t, pieces):
-            if t < 2:
+            if t % 2 == 0:
                 nc.scalar.activation(dss[t][:].indirect(l_n7[:]), pas[t][:], COPY)
             else:
                 nc.vector.tensor_tensor(dss[t][:].indirect(l_n7[:]), pas[t][:], pbs[t][:], ADD)
-            if t == 0:
+            if t == 1:
                 nc.vector.tensor_scalar(halves[t][:, 0:V], dss[t][:, 0:V], -0.5, None, MULT)
                 nc.vector.tensor_tensor(res[:, t, :], halves[t][:].indirect(l_n8[:]), dss[t][:, 0:V], ADD)
             else:

@@ -18,9 +18,18 @@ ADD = mybir.AluOpType.add
 
 P = 128
 PACK = 4
-QUAD = 32
-SPARE = 8
-WIDE = 512 + SPARE
+QUADS = 4
+QUAD = P // QUADS
+ROWS = 4
+BLOCK = QUAD // ROWS
+LIST = 16
+RUN = 4
+WIDE = 512 + 8
+
+A_BANKS_ON_VECTOR = 1
+S_BANKS_ON_SCALAR = 3
+N8_TILE_ON_VECTOR = 1
+SCATTER_TURNS = 2
 
 
 def tile_picked_hkqkindawindfoldd_none_po_kernel(
@@ -33,22 +42,26 @@ def tile_picked_hkqkindawindfoldd_none_po_kernel(
         psum = ctx.enter_context(tc.psum_pool(name="psum", bufs=1))
 
         def load_list(src, name):
-            lst = keep.tile(list(src.shape), U16, name=name)
-            nc.sync.dma_start(lst[:], src)
-            return lst
+            offsets = keep.tile(list(src.shape), U16, name=name)
+            nc.sync.dma_start(offsets[:], src)
+            return offsets
 
         def words_of(packed):
             return packed[0].rearrange("p n t -> p (n t)").bitcast(I32)
 
+        def by_row_tile(column):
+            return column.rearrange("(p t) o -> p (t o)", t=PACK)
+
         def zeroed(engine, width, name):
-            plane = keep.tile([P, width], U8, name=name, align_bytes=64)
-            engine.memset(plane[:].bitcast(I32), 0)
-            return plane
+            tile = keep.tile([P, width], U8, name=name, align_bytes=64)
+            engine.memset(tile[:].bitcast(I32), 0)
+            return tile
 
         def load_scales(queues, plane, scales):
             for q, queue in enumerate(queues):
                 queue.dma_start(
-                    plane[QUAD * q : QUAD * q + 4, :].bitcast(I32), scales[0, 4 * q : 4 * q + 4, :].bitcast(I32)
+                    plane[QUAD * q : QUAD * q + ROWS, :].bitcast(I32),
+                    scales[0, ROWS * q : ROWS * (q + 1), :].bitcast(I32),
                 )
 
         def deal(raw, dtype, name, tag):
@@ -57,6 +70,12 @@ def tile_picked_hkqkindawindfoldd_none_po_kernel(
                 dealt[:].rearrange("p (t m) -> p m t", t=PACK), raw[:].rearrange("p (m t) -> p m t", t=PACK)
             )
             return dealt
+
+        def interleaved(tile):
+            return tile[:].rearrange("p (c i t) -> p c t i", i=RUN, t=PACK)
+
+        def in_runs(tile):
+            return tile[:].rearrange("p t (c i) -> p c t i", i=RUN)
 
         xs = zeroed(nc.gpsimd, T, "xs")
         ws1_raw = zeroed(nc.vector, H, "ws1_raw")
@@ -71,36 +90,39 @@ def tile_picked_hkqkindawindfoldd_none_po_kernel(
         ga_sb = keep.tile([P, PACK], F32, name="ga_sb")
         gb_sb = keep.tile([P, PACK], F32, name="gb_sb")
 
-        l_offs = load_list(offs, "l_offs")
-        l_two = load_list(two, "l_two")
-        nc.sync.dma_start(xs[0:P:8, :].bitcast(I32), x_scales[0].bitcast(I32))
         l_n1 = load_list(n1, "l_n1")
+        l_offs = load_list(offs, "l_offs")
+        nc.sync.dma_start(xs[0:P:BLOCK, :].bitcast(I32), x_scales[0].bitcast(I32))
+        l_two = load_list(two, "l_two")
         nc.sync.dma_start(xw[:].bitcast(I32), words_of(x_words))
+        l_n2 = load_list(n2, "l_n2")
         nc.scalar.dma_start(tabs[0][:, 0:J], tab_rows[:, 0, :])
-        nc.scalar.dma_start(ga_sb[:], ga.rearrange("(p t) o -> p (t o)", t=PACK))
-        load_scales([nc.scalar, nc.sync, nc.sync, nc.sync], ws1_raw, w1_scales)
-        load_scales([nc.gpsimd] * 4, ws2_raw, w2_scales)
+        nc.scalar.dma_start(ga_sb[:], by_row_tile(ga))
+        load_scales([nc.scalar] + [nc.sync] * (QUADS - 1), ws1_raw, w1_scales)
+        load_scales([nc.gpsimd] * QUADS, ws2_raw, w2_scales)
         nc.sync.dma_start(w1_raw[:].bitcast(I32), words_of(w1_words))
-        for t in (1, 2):
+        for t in range(1, PACK - 1):
             nc.sync.dma_start(tabs[t][:, 0:J], tab_rows[:, t, :])
 
         def pick_scales(offsets, plane, name):
             picked = keep.tile([P, S], U8, name=name, tag=name, align_bytes=64)
             nc.vector.tensor_copy(picked[:], xs[:].indirect(offsets[:]))
-            for q in range(4):
+            for q in range(QUADS):
                 nc.sync.dma_start(
-                    plane[QUAD * q : QUAD * q + 4, :].bitcast(I32), picked[QUAD * q : QUAD * (q + 1) : 8, :].bitcast(I32)
+                    plane[QUAD * q : QUAD * q + ROWS, :].bitcast(I32),
+                    picked[QUAD * q : QUAD * (q + 1) : BLOCK, :].bitcast(I32),
                 )
 
-        pick_scales(l_offs, x_plane[:, 0:S], "picked_bytes")
-        nc.sync.dma_start(tabs[3][:, 0:J], tab_rows[:, 3, :])
+        xs_offs = x_plane[:, 0:S]
+        xs_two = x_plane[:, S : S + V]
+        pick_scales(l_offs, xs_offs, "picked_by_offs")
+        nc.sync.dma_start(tabs[PACK - 1][:, 0:J], tab_rows[:, PACK - 1, :])
         nc.sync.dma_start(w2_raw[:].bitcast(I32), words_of(w2_words))
-        pick_scales(l_two, x_plane[:, S : S + V], "picked_by_two")
+        pick_scales(l_two, xs_two, "picked_by_two")
         l_n3 = load_list(n3, "l_n3")
-        nc.sync.dma_start(gb_sb[:], gb.rearrange("(p t) o -> p (t o)", t=PACK))
+        nc.sync.dma_start(gb_sb[:], by_row_tile(gb))
         l_n5 = load_list(n5, "l_n5")
         l_n4 = load_list(n4, "l_n4")
-        l_n2 = load_list(n2, "l_n2")
         l_n7 = load_list(n7, "l_n7")
         l_n6 = load_list(n6, "l_n6")
         l_n8 = load_list(n8, "l_n8")
@@ -112,49 +134,52 @@ def tile_picked_hkqkindawindfoldd_none_po_kernel(
         xw_two = keep.tile([P, V], U32, name="xw_two", tag="w1_raw", align_bytes=64)
         nc.vector.tensor_copy(xw_two[:], xw[:].indirect(l_two[:]))
         w2 = deal(w2_raw, U32, "w2", "w2")
-        ws2 = deal(ws2_raw, U8, "ws2", "picked_bytes")
+        ws2 = deal(ws2_raw, U8, "ws2", "picked_by_offs")
 
-        gtabs = [keep.tile([P, WIDE], F32, name=f"gtab{t}") for t in range(PACK)]
+        ga_tabs = [keep.tile([P, WIDE], F32, name=f"ga_tab{t}") for t in range(PACK)]
         kinds = keep.tile([P, PACK, S], F32, name="kinds")
-        by_n1 = [kinds[:, t, :] for t in range(PACK)]
-        for t in range(PACK):
-            nc.gpsimd.tensor_scalar(gtabs[t][:, 0:J], tabs[t][:, 0:J], ga_sb[:, t : t + 1], 0.0, MULT, ADD)
-        for t in range(PACK):
+        first_by_n1 = keep.tile([P, S], F32, name="first_by_n1")
+        by_n1 = [first_by_n1[:]] + [kinds[:, t, :] for t in range(1, PACK)]
+        for t in range(1, PACK):
+            nc.gpsimd.tensor_scalar(ga_tabs[t][:, 0:J], tabs[t][:, 0:J], ga_sb[:, t : t + 1], 0.0, MULT, ADD)
+        nc.scalar.activation(by_n1[0], tabs[0][:].indirect(l_n1[:]), COPY)
+        nc.scalar.activation(ga_tabs[0][:, 0:J], tabs[0][:, 0:J], COPY, scale=ga_sb[:, 0:1])
+        nc.scalar.activation(kinds[:, 0, :], ga_tabs[0][:].indirect(l_n2[:]), COPY)
+        for t in range(1, PACK):
             nc.scalar.activation(by_n1[t], tabs[t][:].indirect(l_n1[:]), COPY)
 
-        a_banks = [psum.tile([P, S], F32, name=f"a_bank{t}", tag=f"as{t}") for t in range(PACK)]
-        for t in range(PACK):
+        def row_tile_product(bank, t, codes, plane, moving_codes, moving_plane):
             rows = slice(P * t, P * (t + 1))
             nc.tensor.matmul_mx(
-                out=a_banks[t][:], lhsT=w1[:, rows].bitcast(FP8X4), lhsT_scale=ws1[:, rows],
-                rhs=xw_offs[:].bitcast(FP8X4), rhs_scale=x_plane[:, 0:S], start=True, stop=True,
-            )
-        b_banks = [psum.tile([P, V], F32, name=f"b_bank{t}") for t in range(PACK)]
-        for t in range(PACK):
-            rows = slice(P * t, P * (t + 1))
-            nc.tensor.matmul_mx(
-                out=b_banks[t][:], lhsT=w2[:, rows].bitcast(FP8X4), lhsT_scale=ws2[:, rows],
-                rhs=xw_two[:].bitcast(FP8X4), rhs_scale=x_plane[:, S : S + V], start=True, stop=True,
+                out=bank[:], lhsT=codes[:, rows].bitcast(FP8X4), lhsT_scale=plane[:, rows],
+                rhs=moving_codes[:].bitcast(FP8X4), rhs_scale=moving_plane, start=True, stop=True,
             )
 
-        gbs = [keep.tile([P, WIDE], F32, name=f"gb_b{t}") for t in range(PACK)]
-        gas = [keep.tile([P, WIDE], F32, name=f"ga_a{t}") for t in range(PACK)]
+        a_banks = [psum.tile([P, S], F32, name=f"a_bank{t}", tag=f"a_then_s{t}") for t in range(PACK)]
+        for t in range(PACK):
+            row_tile_product(a_banks[t], t, w1, ws1, xw_offs, xs_offs)
+        b_banks = [psum.tile([P, V], F32, name=f"b_bank{t}") for t in range(PACK)]
+        for t in range(PACK):
+            row_tile_product(b_banks[t], t, w2, ws2, xw_two, xs_two)
+
+        gb_bs = [keep.tile([P, WIDE], F32, name=f"gb_b{t}") for t in range(PACK)]
+        ga_as = [keep.tile([P, WIDE], F32, name=f"ga_a{t}") for t in range(PACK)]
         neg5 = keep.tile([P, PACK, V], F32, name="neg5")
         diff = keep.tile([P, PACK, V], F32, name="diff")
         prod = keep.tile([P, PACK, S], F32, name="prod")
         z2 = keep.tile([P, PACK, V], F32, name="z2")
 
         def a_side(t):
-            if t == 0:
-                nc.vector.tensor_scalar(gas[t][:, 0:S], a_banks[t][:], ga_sb[:, t : t + 1], None, MULT)
+            if t < A_BANKS_ON_VECTOR:
+                nc.vector.tensor_scalar(ga_as[t][:, 0:S], a_banks[t][:], ga_sb[:, t : t + 1], None, MULT)
             else:
-                nc.scalar.activation(gas[t][:, 0:S], a_banks[t][:], COPY, scale=ga_sb[:, t : t + 1])
-            nc.vector.tensor_tensor(prod[:, t, :], gas[t][:].indirect(l_n3[:]), by_n1[t], MULT)
+                nc.scalar.activation(ga_as[t][:, 0:S], a_banks[t][:], COPY, scale=ga_sb[:, t : t + 1])
+            nc.vector.tensor_tensor(prod[:, t, :], ga_as[t][:].indirect(l_n3[:]), by_n1[t], MULT)
 
         def b_side(t):
-            nc.scalar.activation(gbs[t][:, 0:V], b_banks[t][:], COPY, scale=gb_sb[:, t : t + 1])
-            nc.scalar.activation(neg5[:, t, :], gbs[t][:].indirect(l_n5[:]), COPY, scale=-1.0)
-            nc.vector.tensor_tensor(diff[:, t, :], gbs[t][:].indirect(l_n4[:]), neg5[:, t, :], ADD)
+            nc.scalar.activation(gb_bs[t][:, 0:V], b_banks[t][:], COPY, scale=gb_sb[:, t : t + 1])
+            nc.scalar.activation(neg5[:, t, :], gb_bs[t][:].indirect(l_n5[:]), COPY, scale=-1.0)
+            nc.vector.tensor_tensor(diff[:, t, :], gb_bs[t][:].indirect(l_n4[:]), neg5[:, t, :], ADD)
             nc.vector.tensor_tensor(z2[:, t, :], b_banks[t][:], diff[:, t, :], MULT)
 
         a_side(0)
@@ -164,9 +189,7 @@ def tile_picked_hkqkindawindfoldd_none_po_kernel(
             b_side(t)
 
         z2_bf = keep.tile([P, V * PACK], BF16, name="z2_bf", align_bytes=64)
-        nc.vector.tensor_copy(
-            z2_bf[:].rearrange("p (c i t) -> p c t i", i=4, t=PACK), z2[:].rearrange("p t (c i) -> p c t i", i=4)
-        )
+        nc.vector.tensor_copy(interleaved(z2_bf), in_runs(z2))
         z2_codes = keep.tile([P, V], U32, name="z2_codes", align_bytes=64)
         z2_plane = keep.tile([P, V], U8, name="z2_plane", align_bytes=64)
         nc.vector.quantize_mx(z2_codes[:].bitcast(FP8X4), z2_plane[:], z2_bf[:])
@@ -176,66 +199,65 @@ def tile_picked_hkqkindawindfoldd_none_po_kernel(
         z_codes = keep.tile([P, S], U32, name="z_codes", align_bytes=64)
         z_plane = keep.tile([P, S], U8, name="z_plane", align_bytes=64)
         s_banks = []
-        for pair in range(2):
-            us = slice(2 * pair, 2 * pair + 2)
-            z_bf = keep.tile([P, 2 * S], BF16, name=f"z_bf{pair}", tag="z_bf", align_bytes=64)
+
+        def sum_z(z_bf, us, ms):
             z_view = z_bf[:].rearrange("p (u m t) -> p m t u", u=2, t=PACK)
-            if pair == 0:
-                for h in range(2):
-                    for t in range(PACK):
-                        nc.scalar.activation(
-                            kinds[:, t, W * h : W * (h + 1)], gtabs[t][:].indirect(l_n2[:, 16 * h : 16 * (h + 1)]), COPY
-                        )
-                    part = slice(64 * h, 64 * (h + 1))
-                    nc.vector.tensor_tensor(z_view[:, part], prod_view[:, part, :, us], kinds_view[:, part, :, us], ADD)
-            else:
-                nc.vector.tensor_tensor(z_view, prod_view[:, :, :, us], kinds_view[:, :, :, us], ADD)
-            for u in range(2):
-                t = 2 * pair + u
-                rows = slice(P * t, P * (t + 1))
-                nc.vector.quantize_mx(z_codes[:, rows].bitcast(FP8X4), z_plane[:, rows], z_bf[:, S * u : S * (u + 1)])
-                s_bank = psum.tile([P, V], F32, name=f"s_bank{t}", tag=f"as{t}")
-                nc.tensor.matmul_mx(
-                    out=s_bank[:], lhsT=z_codes[:, rows].bitcast(FP8X4), lhsT_scale=z_plane[:, rows],
-                    rhs=z2_codes[:].bitcast(FP8X4), rhs_scale=z2_plane[:], start=True, stop=True,
-                )
+            nc.vector.tensor_tensor(z_view[:, ms], prod_view[:, ms, :, us], kinds_view[:, ms, :, us], ADD)
+
+        def multiply_z(z_bf, us):
+            for u in range(us.start, us.stop):
+                rows = slice(P * u, P * (u + 1))
+                values = z_bf[:, PACK * P * (u - us.start) : PACK * P * (u - us.start + 1)]
+                nc.vector.quantize_mx(z_codes[:, rows].bitcast(FP8X4), z_plane[:, rows], values)
+                s_bank = psum.tile([P, V], F32, name=f"s_bank{u}", tag=f"a_then_s{u}")
+                row_tile_product(s_bank, u, z_codes, z_plane, z2_codes, z2_plane[:])
                 s_banks.append(s_bank)
+
+        z_first = keep.tile([P, 2 * PACK * P], BF16, name="z_first", tag="z_bf", align_bytes=64)
+        half = S // 2
+        for h in range(2):
+            entries = l_n2[:, half // LIST * h : half // LIST * (h + 1)]
+            for t in range(1, PACK):
+                nc.scalar.activation(kinds[:, t, half * h : half * (h + 1)], ga_tabs[t][:].indirect(entries), COPY)
+            sum_z(z_first, slice(0, 2), slice(half // PACK * h, half // PACK * (h + 1)))
+        multiply_z(z_first, slice(0, 2))
+        z_second = keep.tile([P, 2 * PACK * P], BF16, name="z_second", tag="z_bf", align_bytes=64)
+        sum_z(z_second, slice(2, PACK), slice(0, P))
+        multiply_z(z_second, slice(2, PACK))
 
         res = keep.tile([P, PACK, V], F32, name="res")
         out_rows = out_0.rearrange("(p t) v -> p t v", t=PACK)
         dss = [keep.tile([P, WIDE], F32, name=f"ds{t}") for t in range(PACK)]
-        pbs = [keep.tile([P, W], F32, name=f"pb{t}") for t in range(PACK)]
-        pas = [keep.tile([P, W], F32, name=f"pa{t}") for t in range(PACK)]
-        halves = [keep.tile([P, WIDE], F32, name=f"half{t}") for t in range(PACK)]
+        neg_pbs = [keep.tile([P, W], F32, name=f"neg_pb{t}") for t in range(PACK)]
+        by_n6 = [keep.tile([P, W], F32, name=f"by_n6_{t}") for t in range(PACK)]
+        neg_halves = [keep.tile([P, WIDE], F32, name=f"neg_half{t}") for t in range(PACK)]
 
         def pair_up(t):
-            if t < 3:
+            if t < S_BANKS_ON_SCALAR:
                 nc.scalar.activation(dss[t][:, 0:V], s_banks[t][:], COPY, scale=0.0625)
             else:
                 nc.vector.tensor_scalar(dss[t][:, 0:V], s_banks[t][:], 0.0625, None, MULT)
-            nc.scalar.activation(pbs[t][:], dss[t][:].indirect(l_n7[:]), COPY, scale=-0.5)
-            if t % 2 == 0:
-                nc.vector.tensor_tensor(pas[t][:], dss[t][:].indirect(l_n6[:]), pbs[t][:], ADD)
+            nc.scalar.activation(neg_pbs[t][:], dss[t][:].indirect(l_n7[:]), COPY, scale=-0.5)
+            if t % SCATTER_TURNS == 0:
+                nc.vector.tensor_tensor(by_n6[t][:], dss[t][:].indirect(l_n6[:]), neg_pbs[t][:], ADD)
             else:
-                nc.vector.tensor_copy(pas[t][:], dss[t][:].indirect(l_n6[:]))
+                nc.vector.tensor_copy(by_n6[t][:], dss[t][:].indirect(l_n6[:]))
 
         def finish(t, pieces):
-            if t % 2 == 0:
-                nc.scalar.activation(dss[t][:].indirect(l_n7[:]), pas[t][:], COPY)
+            if t % SCATTER_TURNS == 0:
+                nc.scalar.activation(dss[t][:].indirect(l_n7[:]), by_n6[t][:], COPY)
             else:
-                nc.vector.tensor_tensor(dss[t][:].indirect(l_n7[:]), pas[t][:], pbs[t][:], ADD)
-            if t == 1:
-                nc.vector.tensor_scalar(halves[t][:, 0:V], dss[t][:, 0:V], -0.5, None, MULT)
-                nc.vector.tensor_tensor(res[:, t, :], halves[t][:].indirect(l_n8[:]), dss[t][:, 0:V], ADD)
+                nc.vector.tensor_tensor(dss[t][:].indirect(l_n7[:]), by_n6[t][:], neg_pbs[t][:], ADD)
+            if t == N8_TILE_ON_VECTOR:
+                nc.vector.tensor_scalar(neg_halves[t][:, 0:V], dss[t][:, 0:V], -0.5, None, MULT)
+                nc.vector.tensor_tensor(res[:, t, :], neg_halves[t][:].indirect(l_n8[:]), dss[t][:, 0:V], ADD)
             else:
                 width = V // pieces
                 for h in range(pieces):
                     cols = slice(width * h, width * (h + 1))
-                    nc.scalar.activation(
-                        halves[t][:, cols], dss[t][:].indirect(l_n8[:, width // 16 * h : width // 16 * (h + 1)]),
-                        COPY, scale=-0.5,
-                    )
-                    nc.vector.tensor_tensor(res[:, t, cols], dss[t][:, cols], halves[t][:, cols], ADD)
+                    entries = l_n8[:, width // LIST * h : width // LIST * (h + 1)]
+                    nc.scalar.activation(neg_halves[t][:, cols], dss[t][:].indirect(entries), COPY, scale=-0.5)
+                    nc.vector.tensor_tensor(res[:, t, cols], dss[t][:, cols], neg_halves[t][:, cols], ADD)
             nc.sync.dma_start(out_rows[:, t, :], res[:, t, :])
 
         pair_up(0)
@@ -244,21 +266,21 @@ def tile_picked_hkqkindawindfoldd_none_po_kernel(
                 pair_up(t + 1)
             finish(t, 2 if t == PACK - 1 else 1)
 
-        o_bf = keep.tile([P, V * PACK], BF16, name="o_bf", align_bytes=64)
-        o_codes = keep.tile([P, V], U32, name="o_codes", align_bytes=64)
-        o_plane = keep.tile([P, V], U8, name="o_plane", align_bytes=64)
-        o_view = o_bf[:].rearrange("p (c i t) -> p c t i", i=4, t=PACK)
-        res_view = res[:].rearrange("p t (c i) -> p c t i", i=4)
-        out_words = out_1[0].rearrange("p n t -> p (n t)").bitcast(I32)
-        nc.scalar.copy(o_view[:, 0:64], res_view[:, 0:64])
-        nc.vector.tensor_copy(o_view[:, 64:128], res_view[:, 64:128])
+        out_bf = keep.tile([P, V * PACK], BF16, name="out_bf", align_bytes=64)
+        out_codes = keep.tile([P, V], U32, name="out_codes", align_bytes=64)
+        out_plane = keep.tile([P, V], U8, name="out_plane", align_bytes=64)
+        out_words = words_of(out_1)
+        half_v = V // 2
+        nc.scalar.copy(interleaved(out_bf)[:, 0 : half_v // RUN], in_runs(res)[:, 0 : half_v // RUN])
+        nc.vector.tensor_copy(interleaved(out_bf)[:, half_v // RUN : V // RUN], in_runs(res)[:, half_v // RUN : V // RUN])
         for h in range(2):
-            cols = slice(W * h, W * (h + 1))
+            cols = slice(half_v * h, half_v * (h + 1))
             nc.vector.quantize_mx(
-                o_codes[:, cols].bitcast(FP8X4), o_plane[:, cols], o_bf[:, PACK * W * h : PACK * W * (h + 1)]
+                out_codes[:, cols].bitcast(FP8X4), out_plane[:, cols], out_bf[:, PACK * cols.start : PACK * cols.stop]
             )
-            nc.sync.dma_start(out_words[:, cols], o_codes[:, cols].bitcast(I32))
-        for q in range(4):
+            nc.sync.dma_start(out_words[:, cols], out_codes[:, cols].bitcast(I32))
+        for q in range(QUADS):
             nc.scalar.dma_start(
-                out_2[0, 4 * q : 4 * q + 4, :].bitcast(I32), o_plane[QUAD * q : QUAD * q + 4, :].bitcast(I32)
+                out_2[0, ROWS * q : ROWS * (q + 1), :].bitcast(I32),
+                out_plane[QUAD * q : QUAD * q + ROWS, :].bitcast(I32),
             )

from contextlib import ExitStack

import concourse.mybir as mybir

K, T, S, V, H, J, W = 512, 2048, 512, 512, 512, 512, 256
FLOPS = 2 * K * H * S + 2 * K * H * V + 2 * H * S * V

F32 = mybir.dt.float32
BF16 = mybir.dt.bfloat16
I32 = mybir.dt.int32
U32 = mybir.dt.uint32
U16 = mybir.dt.uint16
U8 = mybir.dt.uint8
FP8X4 = mybir.dt.float8_e4m3fn_x4
COPY = mybir.ActivationFunctionType.Copy
MULT = mybir.AluOpType.mult
ADD = mybir.AluOpType.add

P = 128
PACK = 4
QUADS = 4
QUAD = P // QUADS
ROWS = 4
BLOCK = QUAD // ROWS
LIST = 16
RUN = 4
WIDE = 512 + 8

A_BANKS_ON_VECTOR = 1
S_BANKS_ON_SCALAR = 3
N8_TILE_ON_VECTOR = 1
SCATTER_TURNS = 2


def tile_picked_hkqkindawindfoldd_none_po_kernel(
    tc, x_words, x_scales, w1_words, w1_scales, w2_words, w2_scales, tab, ga, gb,
    offs, two, n1, n2, n3, n4, n5, n6, n7, n8, out_0, out_1, out_2,
):
    nc = tc.nc
    with ExitStack() as ctx:
        keep = ctx.enter_context(tc.tile_pool(name="keep", bufs=1))
        psum = ctx.enter_context(tc.psum_pool(name="psum", bufs=1))

        def load_list(src, name):
            offsets = keep.tile(list(src.shape), U16, name=name)
            nc.sync.dma_start(offsets[:], src)
            return offsets

        def words_of(packed):
            return packed[0].rearrange("p n t -> p (n t)").bitcast(I32)

        def by_row_tile(column):
            return column.rearrange("(p t) o -> p (t o)", t=PACK)

        def zeroed(engine, width, name):
            tile = keep.tile([P, width], U8, name=name, align_bytes=64)
            engine.memset(tile[:].bitcast(I32), 0)
            return tile

        def load_scales(queues, plane, scales):
            for q, queue in enumerate(queues):
                queue.dma_start(
                    plane[QUAD * q : QUAD * q + ROWS, :].bitcast(I32),
                    scales[0, ROWS * q : ROWS * (q + 1), :].bitcast(I32),
                )

        def deal(raw, dtype, name, tag):
            dealt = keep.tile([P, H], dtype, name=name, tag=tag, align_bytes=64)
            nc.vector.tensor_copy(
                dealt[:].rearrange("p (t m) -> p m t", t=PACK), raw[:].rearrange("p (m t) -> p m t", t=PACK)
            )
            return dealt

        def interleaved(tile):
            return tile[:].rearrange("p (c i t) -> p c t i", i=RUN, t=PACK)

        def in_runs(tile):
            return tile[:].rearrange("p t (c i) -> p c t i", i=RUN)

        xs = zeroed(nc.gpsimd, T, "xs")
        ws1_raw = zeroed(nc.vector, H, "ws1_raw")
        ws2_raw = zeroed(nc.vector, H, "ws2_raw")
        x_plane = zeroed(nc.vector, S + V, "x_plane")

        tab_rows = tab.rearrange("(p t) c -> p t c", t=PACK)
        tabs = [keep.tile([P, WIDE], F32, name=f"tab{t}") for t in range(PACK)]
        w1_raw = keep.tile([P, H], U32, name="w1_raw", tag="w1_raw", align_bytes=64)
        w2_raw = keep.tile([P, H], U32, name="w2_raw")
        xw = keep.tile([P, T], U32, name="xw", align_bytes=64)
        ga_sb = keep.tile([P, PACK], F32, name="ga_sb")
        gb_sb = keep.tile([P, PACK], F32, name="gb_sb")

        l_n1 = load_list(n1, "l_n1")
        l_offs = load_list(offs, "l_offs")
        nc.sync.dma_start(xs[0:P:BLOCK, :].bitcast(I32), x_scales[0].bitcast(I32))
        l_two = load_list(two, "l_two")
        nc.sync.dma_start(xw[:].bitcast(I32), words_of(x_words))
        l_n2 = load_list(n2, "l_n2")
        nc.scalar.dma_start(tabs[0][:, 0:J], tab_rows[:, 0, :])
        nc.scalar.dma_start(ga_sb[:], by_row_tile(ga))
        load_scales([nc.scalar] + [nc.sync] * (QUADS - 1), ws1_raw, w1_scales)
        load_scales([nc.gpsimd] * QUADS, ws2_raw, w2_scales)
        nc.sync.dma_start(w1_raw[:].bitcast(I32), words_of(w1_words))
        for t in range(1, PACK - 1):
            nc.sync.dma_start(tabs[t][:, 0:J], tab_rows[:, t, :])

        def pick_scales(offsets, plane, name):
            picked = keep.tile([P, S], U8, name=name, tag=name, align_bytes=64)
            nc.vector.tensor_copy(picked[:], xs[:].indirect(offsets[:]))
            for q in range(QUADS):
                nc.sync.dma_start(
                    plane[QUAD * q : QUAD * q + ROWS, :].bitcast(I32),
                    picked[QUAD * q : QUAD * (q + 1) : BLOCK, :].bitcast(I32),
                )

        xs_offs = x_plane[:, 0:S]
        xs_two = x_plane[:, S : S + V]
        pick_scales(l_offs, xs_offs, "picked_by_offs")
        nc.sync.dma_start(tabs[PACK - 1][:, 0:J], tab_rows[:, PACK - 1, :])
        nc.sync.dma_start(w2_raw[:].bitcast(I32), words_of(w2_words))
        pick_scales(l_two, xs_two, "picked_by_two")
        l_n3 = load_list(n3, "l_n3")
        nc.sync.dma_start(gb_sb[:], by_row_tile(gb))
        l_n5 = load_list(n5, "l_n5")
        l_n4 = load_list(n4, "l_n4")
        l_n7 = load_list(n7, "l_n7")
        l_n6 = load_list(n6, "l_n6")
        l_n8 = load_list(n8, "l_n8")

        xw_offs = keep.tile([P, S], U32, name="xw_offs", align_bytes=64)
        nc.vector.tensor_copy(xw_offs[:], xw[:].indirect(l_offs[:]))
        ws1 = deal(ws1_raw, U8, "ws1", "ws1")
        w1 = deal(w1_raw, U32, "w1", "w1")
        xw_two = keep.tile([P, V], U32, name="xw_two", tag="w1_raw", align_bytes=64)
        nc.vector.tensor_copy(xw_two[:], xw[:].indirect(l_two[:]))
        w2 = deal(w2_raw, U32, "w2", "w2")
        ws2 = deal(ws2_raw, U8, "ws2", "picked_by_offs")

        ga_tabs = [keep.tile([P, WIDE], F32, name=f"ga_tab{t}") for t in range(PACK)]
        kinds = keep.tile([P, PACK, S], F32, name="kinds")
        first_by_n1 = keep.tile([P, S], F32, name="first_by_n1")
        by_n1 = [first_by_n1[:]] + [kinds[:, t, :] for t in range(1, PACK)]
        for t in range(1, PACK):
            nc.gpsimd.tensor_scalar(ga_tabs[t][:, 0:J], tabs[t][:, 0:J], ga_sb[:, t : t + 1], 0.0, MULT, ADD)
        nc.scalar.activation(by_n1[0], tabs[0][:].indirect(l_n1[:]), COPY)
        nc.scalar.activation(ga_tabs[0][:, 0:J], tabs[0][:, 0:J], COPY, scale=ga_sb[:, 0:1])
        nc.scalar.activation(kinds[:, 0, :], ga_tabs[0][:].indirect(l_n2[:]), COPY)
        for t in range(1, PACK):
            nc.scalar.activation(by_n1[t], tabs[t][:].indirect(l_n1[:]), COPY)

        def row_tile_product(bank, t, codes, plane, moving_codes, moving_plane):
            rows = slice(P * t, P * (t + 1))
            nc.tensor.matmul_mx(
                out=bank[:], lhsT=codes[:, rows].bitcast(FP8X4), lhsT_scale=plane[:, rows],
                rhs=moving_codes[:].bitcast(FP8X4), rhs_scale=moving_plane, start=True, stop=True,
            )

        a_banks = [psum.tile([P, S], F32, name=f"a_bank{t}", tag=f"a_then_s{t}") for t in range(PACK)]
        for t in range(PACK):
            row_tile_product(a_banks[t], t, w1, ws1, xw_offs, xs_offs)
        b_banks = [psum.tile([P, V], F32, name=f"b_bank{t}") for t in range(PACK)]
        for t in range(PACK):
            row_tile_product(b_banks[t], t, w2, ws2, xw_two, xs_two)

        gb_bs = [keep.tile([P, WIDE], F32, name=f"gb_b{t}") for t in range(PACK)]
        ga_as = [keep.tile([P, WIDE], F32, name=f"ga_a{t}") for t in range(PACK)]
        neg5 = keep.tile([P, PACK, V], F32, name="neg5")
        diff = keep.tile([P, PACK, V], F32, name="diff")
        prod = keep.tile([P, PACK, S], F32, name="prod")
        z2 = keep.tile([P, PACK, V], F32, name="z2")

        def a_side(t):
            if t < A_BANKS_ON_VECTOR:
                nc.vector.tensor_scalar(ga_as[t][:, 0:S], a_banks[t][:], ga_sb[:, t : t + 1], None, MULT)
            else:
                nc.scalar.activation(ga_as[t][:, 0:S], a_banks[t][:], COPY, scale=ga_sb[:, t : t + 1])
            nc.vector.tensor_tensor(prod[:, t, :], ga_as[t][:].indirect(l_n3[:]), by_n1[t], MULT)

        def b_side(t):
            nc.scalar.activation(gb_bs[t][:, 0:V], b_banks[t][:], COPY, scale=gb_sb[:, t : t + 1])
            nc.scalar.activation(neg5[:, t, :], gb_bs[t][:].indirect(l_n5[:]), COPY, scale=-1.0)
            nc.vector.tensor_tensor(diff[:, t, :], gb_bs[t][:].indirect(l_n4[:]), neg5[:, t, :], ADD)
            nc.vector.tensor_tensor(z2[:, t, :], b_banks[t][:], diff[:, t, :], MULT)

        a_side(0)
        for t in range(PACK):
            if t + 1 < PACK:
                a_side(t + 1)
            b_side(t)

        z2_bf = keep.tile([P, V * PACK], BF16, name="z2_bf", align_bytes=64)
        nc.vector.tensor_copy(interleaved(z2_bf), in_runs(z2))
        z2_codes = keep.tile([P, V], U32, name="z2_codes", align_bytes=64)
        z2_plane = keep.tile([P, V], U8, name="z2_plane", align_bytes=64)
        nc.vector.quantize_mx(z2_codes[:].bitcast(FP8X4), z2_plane[:], z2_bf[:])

        prod_view = prod[:].rearrange("p t (m u) -> p m t u", u=PACK)
        kinds_view = kinds[:].rearrange("p t (m u) -> p m t u", u=PACK)
        z_codes = keep.tile([P, S], U32, name="z_codes", align_bytes=64)
        z_plane = keep.tile([P, S], U8, name="z_plane", align_bytes=64)
        s_banks = []

        def sum_z(z_bf, us, ms):
            z_view = z_bf[:].rearrange("p (u m t) -> p m t u", u=2, t=PACK)
            nc.vector.tensor_tensor(z_view[:, ms], prod_view[:, ms, :, us], kinds_view[:, ms, :, us], ADD)

        def multiply_z(z_bf, us):
            for u in range(us.start, us.stop):
                rows = slice(P * u, P * (u + 1))
                values = z_bf[:, PACK * P * (u - us.start) : PACK * P * (u - us.start + 1)]
                nc.vector.quantize_mx(z_codes[:, rows].bitcast(FP8X4), z_plane[:, rows], values)
                s_bank = psum.tile([P, V], F32, name=f"s_bank{u}", tag=f"a_then_s{u}")
                row_tile_product(s_bank, u, z_codes, z_plane, z2_codes, z2_plane[:])
                s_banks.append(s_bank)

        z_first = keep.tile([P, 2 * PACK * P], BF16, name="z_first", tag="z_bf", align_bytes=64)
        half = S // 2
        for h in range(2):
            entries = l_n2[:, half // LIST * h : half // LIST * (h + 1)]
            for t in range(1, PACK):
                nc.scalar.activation(kinds[:, t, half * h : half * (h + 1)], ga_tabs[t][:].indirect(entries), COPY)
            sum_z(z_first, slice(0, 2), slice(half // PACK * h, half // PACK * (h + 1)))
        multiply_z(z_first, slice(0, 2))
        z_second = keep.tile([P, 2 * PACK * P], BF16, name="z_second", tag="z_bf", align_bytes=64)
        sum_z(z_second, slice(2, PACK), slice(0, P))
        multiply_z(z_second, slice(2, PACK))

        res = keep.tile([P, PACK, V], F32, name="res")
        out_rows = out_0.rearrange("(p t) v -> p t v", t=PACK)
        dss = [keep.tile([P, WIDE], F32, name=f"ds{t}") for t in range(PACK)]
        neg_pbs = [keep.tile([P, W], F32, name=f"neg_pb{t}") for t in range(PACK)]
        by_n6 = [keep.tile([P, W], F32, name=f"by_n6_{t}") for t in range(PACK)]
        neg_halves = [keep.tile([P, WIDE], F32, name=f"neg_half{t}") for t in range(PACK)]

        def pair_up(t):
            if t < S_BANKS_ON_SCALAR:
                nc.scalar.activation(dss[t][:, 0:V], s_banks[t][:], COPY, scale=0.0625)
            else:
                nc.vector.tensor_scalar(dss[t][:, 0:V], s_banks[t][:], 0.0625, None, MULT)
            nc.scalar.activation(neg_pbs[t][:], dss[t][:].indirect(l_n7[:]), COPY, scale=-0.5)
            if t % SCATTER_TURNS == 0:
                nc.vector.tensor_tensor(by_n6[t][:], dss[t][:].indirect(l_n6[:]), neg_pbs[t][:], ADD)
            else:
                nc.vector.tensor_copy(by_n6[t][:], dss[t][:].indirect(l_n6[:]))

        def finish(t, pieces):
            if t % SCATTER_TURNS == 0:
                nc.scalar.activation(dss[t][:].indirect(l_n7[:]), by_n6[t][:], COPY)
            else:
                nc.vector.tensor_tensor(dss[t][:].indirect(l_n7[:]), by_n6[t][:], neg_pbs[t][:], ADD)
            if t == N8_TILE_ON_VECTOR:
                nc.vector.tensor_scalar(neg_halves[t][:, 0:V], dss[t][:, 0:V], -0.5, None, MULT)
                nc.vector.tensor_tensor(res[:, t, :], neg_halves[t][:].indirect(l_n8[:]), dss[t][:, 0:V], ADD)
            else:
                width = V // pieces
                for h in range(pieces):
                    cols = slice(width * h, width * (h + 1))
                    entries = l_n8[:, width // LIST * h : width // LIST * (h + 1)]
                    nc.scalar.activation(neg_halves[t][:, cols], dss[t][:].indirect(entries), COPY, scale=-0.5)
                    nc.vector.tensor_tensor(res[:, t, cols], dss[t][:, cols], neg_halves[t][:, cols], ADD)
            nc.sync.dma_start(out_rows[:, t, :], res[:, t, :])

        pair_up(0)
        for t in range(PACK):
            if t + 1 < PACK:
                pair_up(t + 1)
            finish(t, 2 if t == PACK - 1 else 1)

        out_bf = keep.tile([P, V * PACK], BF16, name="out_bf", align_bytes=64)
        out_codes = keep.tile([P, V], U32, name="out_codes", align_bytes=64)
        out_plane = keep.tile([P, V], U8, name="out_plane", align_bytes=64)
        out_words = words_of(out_1)
        half_v = V // 2
        nc.scalar.copy(interleaved(out_bf)[:, 0 : half_v // RUN], in_runs(res)[:, 0 : half_v // RUN])
        nc.vector.tensor_copy(interleaved(out_bf)[:, half_v // RUN : V // RUN], in_runs(res)[:, half_v // RUN : V // RUN])
        for h in range(2):
            cols = slice(half_v * h, half_v * (h + 1))
            nc.vector.quantize_mx(
                out_codes[:, cols].bitcast(FP8X4), out_plane[:, cols], out_bf[:, PACK * cols.start : PACK * cols.stop]
            )
            nc.sync.dma_start(out_words[:, cols], out_codes[:, cols].bitcast(I32))
        for q in range(QUADS):
            nc.scalar.dma_start(
                out_2[0, ROWS * q : ROWS * (q + 1), :].bitcast(I32),
                out_plane[QUAD * q : QUAD * q + ROWS, :].bitcast(I32),
            )
